import numpy as np, ml_dtypes
CORES = [6,15,38,47]
N = 4
BF = ml_dtypes.bfloat16
def gentries(a):
    return np.ascontiguousarray(a.reshape(8, 16, -1).transpose(0, 2, 1)).reshape(8, -1)
def gtable(e):
    e = np.asarray(e); return np.ascontiguousarray(e.reshape(8, -1, 16).transpose(0, 2, 1)).reshape(128, -1).astype(np.int32)
R, A, LV, Q = 512, 4, 1, 128
def level(kids, h):
    return kids[h // LV].reshape(8, LV, R, A)[:, h % LV]
def sizes(kids, runs):
    s = [runs[0].astype(np.int64)]
    for h in range(N * LV):
        s.append(np.sum(s[-1][np.arange(8)[:, None, None], level(kids, h)], axis=-1))
    return s
def parts(kids, s, h, n):
    g = np.arange(8)[:, None]; c = level(kids, h)[g, n]
    e = np.add.accumulate(s[h][g[:, :, None], c], axis=-1)
    return c, np.concatenate([np.zeros_like(e[..., :1]), e[..., :-1]], axis=-1)
def put(d, tops, offs):
    d["top"] = np.stack([gtable(v) for v in tops]); d["off"] = np.stack([gtable(v) for v in offs]); return d
def ask(d, tops, u):
    z = sizes(d["kids"], d["runs"])[-1][np.arange(8)[None, :, None], tops]
    return put(d, tops, np.minimum((u * z).astype(np.int64), z - 1))
def setup_inputs(rng):
    d = {"kids": rng.integers(0, R, (N, 8, LV * A * R)).astype(np.int32), "letter": rng.integers(0, 1 << 24, (N, 8, R)).astype(np.int32), "runs": rng.integers(1, 16, (N, 8, R)).astype(np.int32)}
    return ask(d, rng.integers(0, R, (N, 8, Q)), rng.random((N, 8, Q)))
def setup_inputs_edges(rng):
    d = setup_inputs(rng); k = d["kids"]; d["kids"] = np.where(rng.random(k.shape) < 0.25, rng.choice(np.array([0, R - 1]), k.shape), k).astype(np.int32)
    s = sizes(d["kids"], d["runs"]); tops = rng.integers(0, R, (N, 8, Q)); tops[:, :, 0] = 0; tops[:, :, 1] = R - 1; offs = np.zeros((N, 8, Q), np.int64)
    for r in range(N):
        n = tops[r]; low = rng.integers(0, N * LV + 1, (8, Q)); last = rng.integers(0, 2, (8, Q))
        for h in range(N * LV - 1, -1, -1):
            b = np.where(h < low, last * (A - 1), rng.integers(0, A, (8, Q)))[..., None]
            c, w = parts(d["kids"], s, h, n)
            offs[r] += np.take_along_axis(w, b, -1)[..., 0]; n = np.take_along_axis(c, b, -1)[..., 0]
        offs[r] += last * (s[0][np.arange(8)[:, None], n] - 1)
    return put(d, tops, offs)
def setup_inputs_runs(rng):
    d = setup_inputs(rng); d["runs"] = rng.choice(np.array([1, 15]), (N, 8, R)).astype(np.int32); a, b = rng.permutation(8)[:2]
    d["runs"][0, a] = 15; d["runs"][0, b] = 1
    u = rng.random((N, 8, Q)); m = rng.integers(0, 4, u.shape); u = np.where(m == 0, 0.0, np.where(m == 1, 1.0, u))
    return ask(d, rng.integers(0, R, (N, 8, Q)), u)
def setup_inputs_one(rng):
    d = setup_inputs(rng); k = d["kids"].reshape(N, 8, LV * R, A); t = rng.random((N, 8, LV * R, 1)) < 0.5
    d["kids"] = np.where(t, k[..., :1], k).reshape(N, 8, LV * A * R).astype(np.int32)
    tops = np.repeat(rng.integers(0, R, (N, 8, 1)), Q, axis=2); z = sizes(d["kids"], d["runs"])[-1][np.arange(8)[None, :, None], tops]
    start = (rng.random((N, 8, 1)) * z[:, :, :1]).astype(np.int64)
    offs = (start + np.arange(Q)[None, None, :]) % z; q = rng.integers(0, N)
    offs[q] = np.minimum((rng.random((8, 1)) * z[q]).astype(np.int64), z[q] - 1)
    return put(d, tops, offs)
def setup_inputs_spread(rng):
    d = setup_inputs(rng)
    d["kids"] = np.minimum((R * rng.random((N, 8, LV * A * R)) ** 4).astype(np.int32), R - 1)
    d["letter"] = np.minimum(np.exp2(24 * rng.random((N, 8, R))).astype(np.int32), (1 << 24) - 1)
    d["runs"] = np.minimum(1 + (15 * rng.random((N, 8, R)) ** 3).astype(np.int32), 15).astype(np.int32)
    return ask(d, np.minimum((R * rng.random((N, 8, Q)) ** 3).astype(np.int64), R - 1), rng.random((N, 8, Q)) ** 2)
def check_inputs(d):
    bad = []
    for k, lo, hi in (("kids", 0, R - 1), ("letter", 0, (1 << 24) - 1), ("runs", 1, 15), ("top", 0, R - 1)):
        if d[k].min() < lo or d[k].max() > hi: bad.append(k)
    if bad: return bad
    z = sizes(d["kids"], d["runs"])[-1]
    for r in range(N):
        o = gentries(d["off"][r]); n = gentries(d["top"][r])
        if (o < 0).any() or (o >= z[np.arange(8)[:, None], n]).any(): return ["off"]
    return []
def reference(kids, letter, runs, top, off):
    s = sizes(kids, runs); y = np.zeros((N, 8, Q), np.float32)
    for r in range(N):
        n = gentries(top[r]).astype(np.int64); o = gentries(off[r]).astype(np.int64)
        for h in range(N * LV - 1, -1, -1):
            c, w = parts(kids, s, h, n)
            b = np.sum(o[..., None] >= w[..., 1:], axis=-1)[..., None]
            o = o - np.take_along_axis(w, b, -1)[..., 0]; n = np.take_along_axis(c, b, -1)[..., 0]
        y[r] = letter[0][np.arange(8)[:, None], n]
    return {"y": y}

@@ -1,0 +1,397 @@
+from concourse.bass import DstId, RemoteDMATransfer
+from concourse.mybir import AluOpType as Op, ActivationFunctionType as Act
+
+KD = "float16"
+S = "sbuf"
+SCRATCH = {
+    "KI": (S, [128, 2, 16, 4], "int32"), "KF": (S, [128, 2, 4, 16], KD), "ID": (S, [128, 128], KD),
+    "KS": (S, [128, 128], "uint16"), "LL": (S, [128, 128], "uint16"),
+    "RI": (S, [64, 64], "int32"), "RB": (S, [128, 64], "bfloat16"),
+    "QW": (S, [128, 256], "int32"), "QG": (S, [128, 256], "float32"), "QLf": (S, [128, 16], "float32"),
+    "QL": (S, [128, 16], "uint16"), "RQi": (S, [128, 32], "float32"), "RQ": (S, [128, 32], "float32"),
+    "QS": (S, [128, 16], "uint16"), "QA": (S, [128, 4, 8], "uint16"),
+    "PC": (S, [128, 4], "int32"), "PI": (S, [128, 8], "int32"), "PF": (S, [128, 8], "float32"), "PA": (S, [128, 12], "float32"),
+    "DI": (S, [128, 128], "float32"), "JX": (S, [128, 128], "bfloat16"), "TR": (S, [128, 8, 8], "float32"),
+    "IOT": (S, [128, 128], "bfloat16"), "JJ": (S, [128, 128], "bfloat16"), "G16": (S, [128, 128], "bfloat16"),
+    "BLi": (S, [128, 8], "int32"), "BL": (S, [128, 8], "uint16"),
+    "SI": (S, [128, 4, 128], "bfloat16"), "SR": (S, [128, 8, 128], "bfloat16"),
+    "W0": (S, [128, 128], "bfloat16"), "W1": (S, [128, 128], "bfloat16"), "WV": (S, [128, 128], "bfloat16"),
+    "Wa": (S, [128, 128], "bfloat16"), "Wb": (S, [128, 128], "bfloat16"),
+    "A1": (S, [128, 128], "bfloat16"), "A2": (S, [128, 128], "bfloat16"), "A3": (S, [128, 128], "bfloat16"), "A4": (S, [128, 128], "bfloat16"),
+    "DM": (S, [128, 128], "float32"), "BB": (S, [128, 128], "bfloat16"), "BF": (S, [128, 128], "float32"),
+    "SY": (S, [128, 512], "float32"), "T0": (S, [128, 512], "float32"), "T1": (S, [128, 512], "float32"),
+    "T2": (S, [128, 512], "float32"), "V3": (S, [128, 512], "float32"), "V1": (S, [128, 512], "float32"),
+    "X0": (S, [128, 512], "bfloat16"), "X1": (S, [128, 512], "bfloat16"), "X2": (S, [128, 512], "bfloat16"), "X3": (S, [128, 512], "bfloat16"),
+    "LW": (S, [128, 512], "int32"), "LD": ("dram", [4, 128, 8], "int32"), "AD": ("dram", [4, 128, 2], "float32"),
+    "N0": (S, [128, 8], "uint16"), "O0": (S, [128, 8], "float32"), "D1": (S, [128, 128], "float32"), "D2": (S, [128, 128], "bfloat16"),
+    "LG": (S, [128, 128], "float32"), "LT": (S, [128, 128], "float32"), "AN": (S, [128, 8], "float32"), "OI": (S, [128, 8], "int32"),
+}
+for _k in (1, 2):
+    for _n in ("G", "TA", "TT", "M", "SC"):
+        SCRATCH["%s_%d" % (_n, _k)] = (S, [128, 128], "float32")
+    SCRATCH["UI_%d" % _k] = (S, [128, 8], "int32")
+    SCRATCH["NI_%d" % _k] = (S, [128, 8], "int32")
+    SCRATCH["N_%d" % _k] = (S, [128, 8], "uint16")
+for _k in range(8):
+    SCRATCH["ps%d" % _k] = ("psum", [128, 512], "float32")
+SEMAPHORES = ["aL0", "aL1", "aL2", "aL3", "aR", "aQ", "aW", "aLo", "aHi", "snt"] + ["s%d" % _k for _k in range(140)]
+
+
+def rank_program(g, core, T, topo):
+    r = T.rank_of(core)
+    if r is None:
+        return
+    cores = T.cores
+    V, A, P, Y = g.vector, g.scalar, g.tensor, g.sync
+    names = {"g": g, "V": V, "A": A, "P": P, "Y": Y}
+    events = []
+
+    def ev(name=None, count=0):
+        if name is None:
+            name = "s%d" % len([e for e in events if e["auto"]])
+            e = {"sem": T.sem[name], "n": 0, "auto": True, "seen": {}}
+        else:
+            e = {"sem": T.sem[name], "n": count, "auto": False, "seen": {}}
+        events.append(e)
+        return e
+
+    def do(inst, e=None, n=1):
+        if e is None:
+            e = ev()
+        inst.then_inc(e["sem"], n)
+        e["n"] += n
+        return e
+
+    def wait(q, *es):
+        for e in es:
+            if e["seen"].get(q) != e["n"]:
+                names[q].wait_ge(e["sem"], e["n"])
+                e["seen"][q] = e["n"]
+
+    def iota(out, pattern, base, cm, flag=True, e=None):
+        kw = dict(allow_small_or_imprecise_dtypes=True) if flag else {}
+        return do(g.iota(out, pattern, base, cm, **kw), e)
+
+    ps = [T["ps%d" % k] for k in range(8)]
+    others = [s for s in range(4) if s != r]
+
+    def hops(s):
+        a, b = topo.chip(core), topo.chip(cores[s])
+        return 1 if (topo.mates(a, b) or topo.same_plane(a, b)) else 2
+    others.sort(key=lambda s: -hops(s))
+    ne = len(topo.engines(core, cores[others[0]]))
+    snt = ev("snt")
+
+    def send(s, dst, src, sem):
+        rid, pid, _ = topo.addr(cores[s])
+        g.remote_dma(dst, src, T.sem[sem], T.sem.snt, pid, rid, topo.mask(core, cores[s]))
+        snt["n"] += ne
+
+    def shares(s_from):
+        a = topo.chip(cores[s_from])
+        o = [s for s in range(4) if s != s_from]
+        o.sort(key=lambda s: 0 if not (topo.mates(a, topo.chip(cores[s])) or topo.same_plane(a, topo.chip(cores[s]))) else 1)
+        cut = [(0, ne // 2), (ne // 2, 3 * ne // 4), (3 * ne // 4, ne)]
+        return {s: topo.engines(cores[s_from], cores[s])[cut[i][0]:cut[i][1]] for i, s in enumerate(o)}
+
+    def fused(dst_of, src_of, sem):
+        tr = []
+        for s, en in shares(r).items():
+            rid, pid, _ = topo.addr(cores[s])
+            tr.append(RemoteDMATransfer(dst_ids=[DstId(rid=rid, pnc=pid)], dma_engine_mask=sum(1 << e for e in en),
+                                        remote_sem=T.sem[sem], src=src_of(s), dst=dst_of(s)))
+            snt["n"] += len(en)
+        g.remote_dma_fused(tr, local_sem=T.sem.snt)
+
+    aL = [ev("aL%d" % s, ne) if s != r else None for s in range(4)]
+    aR = ev("aR", ne) if r else None
+    aQ = ev("aQ", sum(len(shares(s)[r]) for s in others))
+    aW = ev("aW", len(shares(0)[r])) if r else None
+    aLo = ev("aLo", ne * r) if r > 0 else None
+    aHi = ev("aHi", ne * (3 - r)) if r < 3 else None
+
+    eK = ev()
+    if r == 0:
+        eRI = do(Y.dma_start(T.RI[:], T.runs[:]), None, 16)
+    do(Y.dma_start(T.KI[:, 0], T.kids[0::2, :]), eK, 16)
+    do(A.dma_start(T.KI[:, 1], T.kids[1::2, :]), eK, 16)
+    eQW0 = do(V.memset(T.QW[:], 0))
+    wait("Y", eQW0)
+    eQW = ev()
+    do(Y.dma_start(T.QW[0:8:2, :], T.top[:]), eQW, 16)
+    do(Y.dma_start(T.QW[1:8:2, :], T.off[:]), eQW, 16)
+    if r == 0:
+        eLD = do(Y.dma_start(T.LD[:], T.letter[:]), None, 16)
+
+    ePC = iota(T.PC[:, 0:1], [[0, 1]], 0, 1, False)
+    eDI = iota(T.DI[:], [[1, 128]], 0, -1)
+    eJJ = iota(T.JJ[:], [[0, 8], [1, 16]], 0, 0)
+    eG16 = iota(T.G16[:], [[1, 8], [0, 16]], 0, 0)
+    eTR = iota(T.TR[:], [[1, 8], [8, 2], [0, 4]], 16 * r, -1)
+
+    if r == 0:
+        eRB = do(V.memset(T.RB[64:128, :], 0.0))
+    wait("V", ePC)
+    ePI = ev()
+    pc = T.PC[:, 0:1]
+    do(V.tensor_scalar(T.PI[:, 0:1], pc, 15, None, Op.bitwise_and), ePI)
+    do(V.tensor_scalar(T.PI[:, 1:2], pc, 4, 3, Op.logical_shift_right, Op.bitwise_and), ePI)
+    do(V.tensor_scalar(T.PI[:, 2:3], pc, 3, None, Op.bitwise_and), ePI)
+    do(V.tensor_scalar(T.PI[:, 3:4], pc, 4, None, Op.logical_shift_right), ePI)
+    do(V.tensor_scalar(T.PI[:, 4:5], pc, 7, None, Op.bitwise_and), ePI)
+    do(V.tensor_scalar(T.PI[:, 5:6], pc, 3, 1, Op.logical_shift_right, Op.bitwise_and), ePI)
+    wait("V", ePI)
+    ePF = do(V.tensor_copy(T.PF[:, 0:6], T.PI[:, 0:6]))
+    wait("V", eDI)
+    eID = do(V.tensor_scalar(T.ID[:], T.DI[:], 0.0, None, Op.is_equal))
+    eSR0 = do(V.memset(T.SR[0:64], 0.0))
+
+    def selectors():
+        e0 = do(V.memset(T.SI[:], 0.0))
+        wait("V", eTR, eSR0)
+        eR = do(V.tensor_scalar(T.SR[0:64, :, 0::16], T.TR[0:64], 0.0, None, Op.is_equal))
+        wait("V", e0)
+        eI = ev()
+        do(V.memset(T.SI[0:1, :, 1::16], 16.0), eI)
+        do(V.memset(T.SI[32:33, :, 2::16], 1.0), eI)
+        for q in range(1, 4):
+            do(V.memset(T.SI[64:65, q, 1::16], 128.0 * q), eI)
+        return eR, eI
+    if r:
+        eSR, eSI = selectors()
+
+    pj, pcc, pd, pg, p7, p8 = [T.PF[:, i:i + 1] for i in range(6)]
+    a0, aV, s1, sN, sV, sC, sCn, fq, sg = [T.PA[:, i:i + 1] for i in range(9)]
+    wait("A", ePF)
+    esg = do(A.activation(sg, pj, Act.Sign, bias=3.5, scale=-1.0))
+    ePA = ev()
+    do(A.activation(fq, p7, Act.Identity, bias=p8, scale=16.0), ePA)
+    do(A.activation(a0, pj, Act.Identity, bias=pcc, scale=4.0), ePA)
+    do(A.activation(aV, pcc, Act.Identity, bias=pd, scale=4.0), ePA)
+    wait("A", esg)
+    for col, sc, bi in ((s1, 0.5, 0.5), (sN, -0.5, -0.5), (sV, -256.0, -256.0), (sC, -0.5, 0.5), (sCn, 0.5, -0.5)):
+        do(A.activation(col, sg, Act.Identity, bias=bi, scale=sc), ePA)
+    wait("A", eJJ, eG16)
+    eIO = ev()
+    do(A.activation(T.IOT[0:32, :], T.G16[0:32, :], Act.Copy), eIO)
+    do(A.activation(T.IOT[32:64, :], T.JJ[32:64, :], Act.Copy), eIO)
+    do(A.activation(T.IOT[64:128, :], T.JJ[64:128, :], Act.Identity, bias=1.0, scale=0.0), eIO)
+    eJX = ev()
+    for a, b in ((0, 0), (64, 64)):
+        do(A.activation(T.JX[a:a + 64, b:b + 64], T.JJ[a:a + 64, b:b + 64], Act.Copy), eJX)
+    for a, b in ((0, 64), (64, 0)):
+        do(A.activation(T.JX[a:a + 64, b:b + 64], T.JJ[a:a + 64, b:b + 64], Act.Identity, bias=-64.0, scale=1.0), eJX)
+    wait("A", ePA, eJX)
+    e1 = do(A.activation(T.A1[:], T.JX[:], Act.Abs))
+    e2 = do(A.activation(T.A2[:], T.JX[:], Act.Abs, bias=aV, scale=-1.0))
+    e3 = do(A.activation(T.A3[:], T.JJ[:], Act.Abs, bias=pj, scale=-1.0))
+    e4 = do(A.activation(T.A4[:], T.G16[:], Act.Abs, bias=pg, scale=-1.0))
+    wait("A", e2)
+    eWb = do(A.activation(T.Wb[:], T.A2[:], Act.Relu, bias=sC, scale=sCn))
+    wait("A", e1)
+    eB = ev()
+    do(A.activation(T.W1[:], T.A1[:], Act.Relu, bias=s1, scale=sN), eB)
+    wait("A", e3)
+    eDM = do(A.activation(T.DM[:], T.A3[:], Act.Relu, bias=1.0, scale=-1.0))
+    wait("A", e4)
+    do(A.activation(T.BB[:], T.A4[:], Act.Relu, bias=512.0, scale=-512.0), eB)
+    do(A.activation(T.BF[:], T.A4[:], Act.Relu, bias=512.0, scale=-512.0), eB)
+
+    if r == 0:
+        wait("V", eRI)
+        do(V.tensor_copy(T.RB[0:64, :], T.RI[:]), eRB)
+        wait("g", eRB)
+        ids = [DstId(rid=topo.addr(cores[s])[0], pnc=topo.addr(cores[s])[1]) for s in others]
+        g.remote_dma_fused([RemoteDMATransfer(dst_ids=ids, dma_engine_mask=topo.mask(core, cores[others[0]]), remote_sem=T.sem.aR,
+                                              srcs=[T.RB[:]], dsts=[T.RB[:] for s in others])], local_sem=T.sem.snt)
+        snt["n"] += ne
+        aR = eRB
+    eQLf = ev()
+    for h in range(2):
+        iota(T.QLf[:, 8 * h:8 * h + 8], [[128, 2], [4, 2], [8, 2]], 2 * h, 0, True, eQLf)
+    eRQi = iota(T.RQi[:], [[-1, 2], [1, 16]], 0, -2)
+
+    wait("V", eK)
+    eKF = ev()
+    for c in range(4):
+        do(V.tensor_copy(T.KF[:, :, c, :], T.KI[:, :, :, c]), eKF)
+    wait("P", eID, eKF)
+    e = do(P.matmul(ps[4][:, 0:128], T.KF[:], T.ID[:], True, True))
+    wait("V", e)
+    eKS = do(V.tensor_copy(T.KS[:], ps[4][:, 0:128]))
+    wait("g", eKS)
+    for s in others:
+        send(s, T.LL[:, 32 * r:32 * r + 32], T.KS[:, 32 * s:32 * s + 32], "aL%d" % r)
+    aL[r] = eKS
+    eBLi = iota(T.BLi[:], [[1, 8]], 0, 0, False)
+
+    wait("V", eQLf, ePA)
+    eQL = do(V.tensor_scalar(T.QL[:], T.QLf[:], fq, None, Op.add))
+    wait("V", eRQi)
+    eRQ = do(V.tensor_scalar(T.RQ[:], T.RQi[:], 0.0, None, Op.is_equal))
+    wait("V", eQL, eQW)
+    eQG = do(V.tensor_copy(T.QG[:], T.QW[:].indirect(T.QL[:])))
+    if r == 0:
+        eSR, eSI = selectors()
+
+    def numbers():
+        for q in range(4):
+            P.matmul(ps[q][:, 0:128], T.SI[:, q, :], T.IOT[:], True, False)
+    if r:
+        wait("P", eIO, eSI)
+        numbers()
+    wait("P", eQG, eRQ)
+    P.matmul(ps[5][:, 0:16], T.QG[0:8, 0:128], T.RQ[0:8, 0:16], True, False)
+    e = do(P.matmul(ps[5][:, 0:16], T.QG[0:8, 128:256], T.RQ[0:8, 16:32], False, True))
+    if r == 0:
+        wait("P", eIO, eSI)
+        numbers()
+    wait("V", eJX)
+    eW0 = do(V.tensor_scalar(T.W0[:], T.JX[:], a0, None, Op.is_equal))
+    eWa = do(V.tensor_scalar(T.Wa[:], T.JX[:], aV, sV, Op.is_gt, Op.mult))
+    wait("V", e)
+    eQS = ev()
+    do(V.tensor_copy(T.QS[:], ps[5][:, 0:16]), eQS)
+    do(V.tensor_copy(T.QA[:, r, 0:4], ps[5][:, 4 * r:4 * r + 4]), eQS)
+    wait("V", eWa, eWb)
+    eWV = do(V.tensor_tensor(T.WV[:], T.Wa[:], T.Wb[:], Op.add))
+    wait("V", eBLi)
+    eBL = do(V.tensor_copy(T.BL[:], T.BLi[:]))
+    wait("g", eQS)
+    fused(lambda s: T.QA[:, r, 0:4], lambda s: T.QS[:, 4 * s:4 * s + 4], "aQ")
+    if r == 0:
+        wait("g", eLD)
+        fused(lambda s: T.LD[s], lambda s: T.LD[s], "aW")
+    eLW0 = iota(T.LW[:], [[0, 512]], 0, 0, False)
+    wait("Y", eLW0)
+    if r:
+        wait("Y", aW)
+    eLW = ev()
+    for q in range(4):
+        do(Y.dma_start(T.LW[16 * q::64, :], T.LD[r] if r else T.letter[0:2, :]), eLW, 16)
+
+    def copy(q, out, in_, e=None):
+        return do(V.tensor_copy(out, in_) if q == "V" else A.activation(out, in_, Act.Copy), e)
+
+    order = (0, 2, 1, 3)
+    eng = "VVAA"
+
+    def copies(win, banks, em, who=eng):
+        e = ev()
+        for q in order:
+            wait(who[q], em[q])
+            copy(who[q], win[:, 128 * q:128 * q + 128], banks[q][:, 0:128], e)
+        return e
+
+    wait("P", eSR, aR)
+    em = {}
+    for q in order:
+        for b in (2 * q, 2 * q + 1):
+            m = P.matmul(ps[q][:, 64 * (b % 2):64 * (b % 2) + 64], T.SR[0:64, b, :], T.RB[0:64, :], False, b % 2 == 1)
+        em[q] = do(m)
+    eSY = copies(T.SY, ps[0:4], em)
+
+    def level(h, win, ew, X, Wt, banks, first):
+        lists = T.KS if h == r else T.LL
+        eg = {}
+        for q in order:
+            wait(eng[q], aL[h], ew)
+            eg[q] = copy(eng[q], X[:, 128 * q:128 * q + 128], win[:].indirect(lists[:, 32 * h + 8 * q:32 * h + 8 * q + 8]))
+        em = {}
+        for q in order:
+            wait("P", eg[q])
+            em[q] = do(P.matmul(banks[q][:, 0:128], Wt[:], X[:, 128 * q:128 * q + 128], first, True))
+        return em
+
+    wait("P", eW0, eWV, eB, eKS, eQS)
+    em = level(0, T.SY, eSY, T.X0, T.W0, ps[4:8], True)
+    eT0 = copies(T.T0, ps[4:8], em)
+    wait("P", eSY)
+    numbers()
+    em = level(1, T.T0, eT0, T.X1, T.W1, ps[0:4], False)
+    eT1 = copies(T.T1, ps[0:4], em)
+    wait("P", eT0)
+    eVm = ev()
+    do(P.matmul(ps[6][:, 256:512], T.WV[:], T.X1[:, 0:256], True, True), eVm)
+    do(P.matmul(ps[7][:, 256:512], T.WV[:], T.X1[:, 256:512], True, True), eVm)
+    em = level(2, T.T1, eT1, T.X2, T.W0, ps[4:8], True)
+    eT2 = copies(T.T2, ps[4:8], em, "VAAA")
+    wait("V", aQ, eQS)
+    eO0 = do(V.tensor_copy(T.O0[:], T.QA[:, :, 2:4]))
+    eN0 = do(V.tensor_copy(T.N0[:], T.QA[:, :, 0:2]))
+    wait("V", eO0, eBL, eDM)
+    eD1 = do(V.tensor_tensor(T.D1[:], T.O0[:].indirect(T.BL[:]), T.DM[:], Op.mult))
+    wait("P", eT1, eT2, eD1)
+    eZ = [do(P.matmul(ps[4][:, 0:64], T.BF[:], T.D1[:, 0:64], True, True))]
+    em = level(3, T.T2, eT2, T.X3, T.WV, ps[0:4], True)
+    eZ.append(do(P.matmul(ps[5][:, 0:64], T.BF[:], T.D1[:, 64:128], True, True)))
+    eV3 = copies(T.V3, ps[0:4], em)
+
+    H = (slice(0, 64), slice(64, 128))
+
+    def pick(k, eG, eZ, z):
+        G, TA, TT, M, SC, UI, NI, N = [T["%s_%d" % (n, k)] for n in ("G", "TA", "TT", "M", "SC", "UI", "NI", "N")]
+        e = [None, None]
+        for h in range(2):
+            wait("V", eG[h], eZ[h])
+            e[h] = do(V.tensor_tensor(TA[:, H[h]], G[:, H[h]], z[h][:, 0:64], Op.add))
+        for h in range(2):
+            wait("V", e[h])
+            e[h] = do(V.transpose(TT[:, H[h]], TA[:, H[h]]))
+        for h in range(2):
+            wait("V", e[h])
+            e[h] = do(V.tensor_scalar(M[:, H[h]], TT[:, H[h]], 0.0, None, Op.is_lt))
+        eS = ev()
+        for h in range(2):
+            wait("V", e[h])
+            do(V.tensor_tensor_scan(SC[:, H[h]], M[:, H[h]], TT[:, H[h]], 0.0, Op.mult, Op.max), eS)
+        wait("V", eS)
+        eU = do(V.tensor_copy(UI[:], SC[:, 15::16]))
+        wait("V", eU)
+        e = do(V.tensor_scalar(NI[:], UI[:], 511, None, Op.bitwise_and))
+        eO = do(V.tensor_scalar(T.OI[:], UI[:], 9, None, Op.logical_shift_right)) if k == 1 else None
+        wait("V", e)
+        return do(V.tensor_copy(N[:], NI[:])), eO
+
+    wait("V", eV3, eN0)
+    wait("A", eV3, eN0)
+    eG = [copy("VA"[h], T.G_1[:, H[h]], T.V3[:].indirect(T.N0[:, 4 * h:4 * h + 4])) for h in range(2)]
+    eV1 = ev()
+    wait("A", eVm, eT2)
+    copy("A", T.V1[:, 0:256], ps[6][:, 256:512], eV1)
+    copy("A", T.V1[:, 256:512], ps[7][:, 256:512], eV1)
+    eN, eO = pick(1, eG, eZ, ps[4:6])
+    wait("A", eV1, eN)
+    eG = [copy("A", T.G_2[:, H[h]], T.V1[:].indirect(T.N_1[:, 4 * h:4 * h + 4])) for h in range(2)]
+    wait("V", eO)
+    wait("P", eV3)
+    eZ = []
+    for h in range(2):
+        e = do(V.tensor_tensor(T.D2[:, H[h]], T.OI[:].indirect(T.BL[:, 4 * h:4 * h + 4]), T.DM[:, H[h]], Op.mult))
+        wait("P", e)
+        eZ.append(do(P.matmul(ps[h][:, 0:64], T.BB[:], T.D2[:, H[h]], True, True)))
+    eN, _ = pick(2, eG, eZ, ps[0:2])
+    wait("V", eLW, eN)
+    e = do(V.tensor_copy(T.LG[:], T.LW[:].indirect(T.N_2[:])))
+    wait("V", e)
+    e = do(V.transpose(T.LT[:], T.LG[:]))
+    wait("V", e)
+    eAN = do(V.tensor_copy(T.AN[:], T.LT[:, 0::16]))
+    wait("g", eAN)
+    for s in others:
+        send(s, T.AD[r], T.AN[:, 2 * s:2 * s + 2], "aLo" if r < s else "aHi")
+    wait("Y", eAN)
+    eY = do(Y.dma_start(T.y[2 * r:2 * r + 2, :], T.AN[:, 2 * r:2 * r + 2]), None, 16)
+    if r > 0:
+        wait("A", aLo)
+        e = do(A.dma_start(T.y[0:2 * r, :], T.AD[0:r]), None, 16)
+        wait("A", e)
+    if r < 3:
+        q = "Y" if r > 0 else "A"
+        wait(q, aHi)
+        e = do(names[q].dma_start(T.y[2 * r + 2:8, :], T.AD[r + 1:4]), None, 16)
+        wait(q, e)
+    wait("Y", eY)
+    for e in events:
+        if e["n"] and e["n"] not in e["seen"].values():
+            wait("g", e)

@@ -1,35 +1,30 @@
 from concourse.bass import DstId, RemoteDMATransfer
 from concourse.mybir import AluOpType as Op, ActivationFunctionType as Act
 
-KD = "float16"
 S = "sbuf"
 SCRATCH = {
-    "KI": (S, [128, 2, 16, 4], "int32"), "KF": (S, [128, 2, 4, 16], KD), "ID": (S, [128, 128], KD),
+    "KI": (S, [128, 2, 16, 4], "int32"), "KF": (S, [128, 2, 4, 16], "float16"), "ID": (S, [128, 128], "float16"),
     "KS": (S, [128, 128], "uint16"), "LL": (S, [128, 128], "uint16"),
     "RI": (S, [64, 64], "int32"), "RB": (S, [128, 64], "bfloat16"),
     "QW": (S, [128, 256], "int32"), "QG": (S, [128, 256], "float32"), "QLf": (S, [128, 16], "float32"),
     "QL": (S, [128, 16], "uint16"), "RQi": (S, [128, 32], "float32"), "RQ": (S, [128, 32], "float32"),
     "QS": (S, [128, 16], "uint16"), "QA": (S, [128, 4, 8], "uint16"),
     "PC": (S, [128, 4], "int32"), "PI": (S, [128, 8], "int32"), "PF": (S, [128, 8], "float32"), "PA": (S, [128, 12], "float32"),
-    "DI": (S, [128, 128], "float32"), "JX": (S, [128, 128], "bfloat16"), "TR": (S, [128, 8, 8], "float32"),
-    "IOT": (S, [128, 128], "bfloat16"), "JJ": (S, [128, 128], "bfloat16"), "G16": (S, [128, 128], "bfloat16"),
-    "BLi": (S, [128, 8], "int32"), "BL": (S, [128, 8], "uint16"),
+    "TR": (S, [128, 8, 8], "float32"), "BLi": (S, [128, 8], "int32"), "BL": (S, [128, 8], "uint16"),
     "SI": (S, [128, 4, 128], "bfloat16"), "SR": (S, [128, 8, 128], "bfloat16"),
-    "W0": (S, [128, 128], "bfloat16"), "W1": (S, [128, 128], "bfloat16"), "WV": (S, [128, 128], "bfloat16"),
-    "Wa": (S, [128, 128], "bfloat16"), "Wb": (S, [128, 128], "bfloat16"),
-    "A1": (S, [128, 128], "bfloat16"), "A2": (S, [128, 128], "bfloat16"), "A3": (S, [128, 128], "bfloat16"), "A4": (S, [128, 128], "bfloat16"),
-    "DM": (S, [128, 128], "float32"), "BB": (S, [128, 128], "bfloat16"), "BF": (S, [128, 128], "float32"),
-    "SY": (S, [128, 512], "float32"), "T0": (S, [128, 512], "float32"), "T1": (S, [128, 512], "float32"),
-    "T2": (S, [128, 512], "float32"), "V3": (S, [128, 512], "float32"), "V1": (S, [128, 512], "float32"),
-    "X0": (S, [128, 512], "bfloat16"), "X1": (S, [128, 512], "bfloat16"), "X2": (S, [128, 512], "bfloat16"), "X3": (S, [128, 512], "bfloat16"),
     "LW": (S, [128, 512], "int32"), "LD": ("dram", [4, 128, 8], "int32"), "AD": ("dram", [4, 128, 2], "float32"),
-    "N0": (S, [128, 8], "uint16"), "O0": (S, [128, 8], "float32"), "D1": (S, [128, 128], "float32"), "D2": (S, [128, 128], "bfloat16"),
-    "LG": (S, [128, 128], "float32"), "LT": (S, [128, 128], "float32"), "AN": (S, [128, 8], "float32"), "OI": (S, [128, 8], "int32"),
+    "N0": (S, [128, 8], "uint16"), "O0": (S, [128, 8], "float32"), "OI": (S, [128, 8], "int32"),
 }
+for _n in "JX IOT JJ G16 W0 W1 WV Wa Wb A1 A2 A3 A4 BB D2".split():
+    SCRATCH[_n] = (S, [128, 128], "bfloat16")
+for _n in "DI DM BF D1 LG LT G_1 TA_1 TT_1 M_1 G_2 TA_2 TT_2 M_2".split():
+    SCRATCH[_n] = (S, [128, 128], "float32")
+for _n in "SY T0 T1 T2 V3 V1".split():
+    SCRATCH[_n] = (S, [128, 512], "float32")
+for _n in "X0 X1 X2 X3".split():
+    SCRATCH[_n] = (S, [128, 512], "bfloat16")
 for _k in (1, 2):
-    for _n in ("G", "TA", "TT", "M", "SC"):
-        SCRATCH["%s_%d" % (_n, _k)] = (S, [128, 128], "float32")
-    SCRATCH["UI_%d" % _k] = (S, [128, 8], "int32")
+    SCRATCH["SC_%d" % _k] = (S, [128, 128], "int32")
     SCRATCH["NI_%d" % _k] = (S, [128, 8], "int32")
     SCRATCH["N_%d" % _k] = (S, [128, 8], "uint16")
 for _k in range(8):
@@ -47,13 +42,11 @@ def rank_program(g, core, T, topo):
     events = []
 
     def ev(name=None, count=0):
-        if name is None:
+        auto = name is None
+        if auto:
             name = "s%d" % len([e for e in events if e["auto"]])
-            e = {"sem": T.sem[name], "n": 0, "auto": True, "seen": {}}
-        else:
-            e = {"sem": T.sem[name], "n": count, "auto": False, "seen": {}}
-        events.append(e)
-        return e
+        events.append({"sem": T.sem[name], "n": count, "auto": auto, "seen": {}})
+        return events[-1]
 
     def do(inst, e=None, n=1):
         if e is None:
@@ -73,46 +66,45 @@ def rank_program(g, core, T, topo):
         return do(g.iota(out, pattern, base, cm, **kw), e)
 
     ps = [T["ps%d" % k] for k in range(8)]
-    others = [s for s in range(4) if s != r]
 
-    def hops(s):
-        a, b = topo.chip(core), topo.chip(cores[s])
-        return 1 if (topo.mates(a, b) or topo.same_plane(a, b)) else 2
-    others.sort(key=lambda s: -hops(s))
+    def far_first(f):
+        a = topo.chip(cores[f])
+        near = lambda s: topo.mates(a, topo.chip(cores[s])) or topo.same_plane(a, topo.chip(cores[s]))
+        return sorted([s for s in range(4) if s != f], key=near)
+    others = far_first(r)
     ne = len(topo.engines(core, cores[others[0]]))
     snt = ev("snt")
 
-    def send(s, dst, src, sem):
-        rid, pid, _ = topo.addr(cores[s])
-        g.remote_dma(dst, src, T.sem[sem], T.sem.snt, pid, rid, topo.mask(core, cores[s]))
-        snt["n"] += ne
-
-    def shares(s_from):
-        a = topo.chip(cores[s_from])
-        o = [s for s in range(4) if s != s_from]
-        o.sort(key=lambda s: 0 if not (topo.mates(a, topo.chip(cores[s])) or topo.same_plane(a, topo.chip(cores[s]))) else 1)
+    def shares(f):
         cut = [(0, ne // 2), (ne // 2, 3 * ne // 4), (3 * ne // 4, ne)]
-        return {s: topo.engines(cores[s_from], cores[s])[cut[i][0]:cut[i][1]] for i, s in enumerate(o)}
+        return {s: topo.engines(cores[f], cores[s])[cut[i][0]:cut[i][1]] for i, s in enumerate(far_first(f))}
 
-    def fused(dst_of, src_of, sem):
+    def send(dst_of, src_of, sem_of, fuse, only=range(4)):
         tr = []
         for s, en in shares(r).items():
+            if s not in only:
+                continue
             rid, pid, _ = topo.addr(cores[s])
-            tr.append(RemoteDMATransfer(dst_ids=[DstId(rid=rid, pnc=pid)], dma_engine_mask=sum(1 << e for e in en),
-                                        remote_sem=T.sem[sem], src=src_of(s), dst=dst_of(s)))
-            snt["n"] += len(en)
-        g.remote_dma_fused(tr, local_sem=T.sem.snt)
+            if fuse:
+                tr.append(RemoteDMATransfer(dst_ids=[DstId(rid=rid, pnc=pid)], dma_engine_mask=sum(1 << e for e in en),
+                                            remote_sem=T.sem[sem_of(s)], src=src_of(s), dst=dst_of(s)))
+            else:
+                g.remote_dma(dst_of(s), src_of(s), T.sem[sem_of(s)], T.sem.snt, pid, rid, topo.mask(core, cores[s]))
+            snt["n"] += len(en) if fuse else ne
+        if fuse:
+            g.remote_dma_fused(tr, local_sem=T.sem.snt)
 
     aL = [ev("aL%d" % s, ne) if s != r else None for s in range(4)]
     aR = ev("aR", ne) if r else None
     aQ = ev("aQ", sum(len(shares(s)[r]) for s in others))
     aW = ev("aW", len(shares(0)[r])) if r else None
-    aLo = ev("aLo", ne * r) if r > 0 else None
-    aHi = ev("aHi", ne * (3 - r)) if r < 3 else None
+    aLo = ev("aLo", ne * r)
+    aHi = ev("aHi", ne * (3 - r))
 
     eK = ev()
     if r == 0:
         eRI = do(Y.dma_start(T.RI[:], T.runs[:]), None, 16)
+        eRB = do(V.memset(T.RB[64:128, :], 0.0))
     do(Y.dma_start(T.KI[:, 0], T.kids[0::2, :]), eK, 16)
     do(A.dma_start(T.KI[:, 1], T.kids[1::2, :]), eK, 16)
     eQW0 = do(V.memset(T.QW[:], 0))
@@ -126,76 +118,17 @@ def rank_program(g, core, T, topo):
     ePC = iota(T.PC[:, 0:1], [[0, 1]], 0, 1, False)
     eDI = iota(T.DI[:], [[1, 128]], 0, -1)
     eJJ = iota(T.JJ[:], [[0, 8], [1, 16]], 0, 0)
-    eG16 = iota(T.G16[:], [[1, 8], [0, 16]], 0, 0)
-    eTR = iota(T.TR[:], [[1, 8], [8, 2], [0, 4]], 16 * r, -1)
 
-    if r == 0:
-        eRB = do(V.memset(T.RB[64:128, :], 0.0))
     wait("V", ePC)
     ePI = ev()
     pc = T.PC[:, 0:1]
-    do(V.tensor_scalar(T.PI[:, 0:1], pc, 15, None, Op.bitwise_and), ePI)
-    do(V.tensor_scalar(T.PI[:, 1:2], pc, 4, 3, Op.logical_shift_right, Op.bitwise_and), ePI)
-    do(V.tensor_scalar(T.PI[:, 2:3], pc, 3, None, Op.bitwise_and), ePI)
-    do(V.tensor_scalar(T.PI[:, 3:4], pc, 4, None, Op.logical_shift_right), ePI)
-    do(V.tensor_scalar(T.PI[:, 4:5], pc, 7, None, Op.bitwise_and), ePI)
-    do(V.tensor_scalar(T.PI[:, 5:6], pc, 3, 1, Op.logical_shift_right, Op.bitwise_and), ePI)
-    wait("V", ePI)
-    ePF = do(V.tensor_copy(T.PF[:, 0:6], T.PI[:, 0:6]))
+    shr, band = Op.logical_shift_right, Op.bitwise_and
+    for i, a in enumerate(((15, None, band), (4, 3, shr, band), (3, None, band), (4, None, shr), (7, None, band), (3, 1, shr, band))):
+        do(V.tensor_scalar(T.PI[:, i:i + 1], pc, *a), ePI)
     wait("V", eDI)
     eID = do(V.tensor_scalar(T.ID[:], T.DI[:], 0.0, None, Op.is_equal))
-    eSR0 = do(V.memset(T.SR[0:64], 0.0))
-
-    def selectors():
-        e0 = do(V.memset(T.SI[:], 0.0))
-        wait("V", eTR, eSR0)
-        eR = do(V.tensor_scalar(T.SR[0:64, :, 0::16], T.TR[0:64], 0.0, None, Op.is_equal))
-        wait("V", e0)
-        eI = ev()
-        do(V.memset(T.SI[0:1, :, 1::16], 16.0), eI)
-        do(V.memset(T.SI[32:33, :, 2::16], 1.0), eI)
-        for q in range(1, 4):
-            do(V.memset(T.SI[64:65, q, 1::16], 128.0 * q), eI)
-        return eR, eI
-    if r:
-        eSR, eSI = selectors()
-
-    pj, pcc, pd, pg, p7, p8 = [T.PF[:, i:i + 1] for i in range(6)]
-    a0, aV, s1, sN, sV, sC, sCn, fq, sg = [T.PA[:, i:i + 1] for i in range(9)]
-    wait("A", ePF)
-    esg = do(A.activation(sg, pj, Act.Sign, bias=3.5, scale=-1.0))
-    ePA = ev()
-    do(A.activation(fq, p7, Act.Identity, bias=p8, scale=16.0), ePA)
-    do(A.activation(a0, pj, Act.Identity, bias=pcc, scale=4.0), ePA)
-    do(A.activation(aV, pcc, Act.Identity, bias=pd, scale=4.0), ePA)
-    wait("A", esg)
-    for col, sc, bi in ((s1, 0.5, 0.5), (sN, -0.5, -0.5), (sV, -256.0, -256.0), (sC, -0.5, 0.5), (sCn, 0.5, -0.5)):
-        do(A.activation(col, sg, Act.Identity, bias=bi, scale=sc), ePA)
-    wait("A", eJJ, eG16)
-    eIO = ev()
-    do(A.activation(T.IOT[0:32, :], T.G16[0:32, :], Act.Copy), eIO)
-    do(A.activation(T.IOT[32:64, :], T.JJ[32:64, :], Act.Copy), eIO)
-    do(A.activation(T.IOT[64:128, :], T.JJ[64:128, :], Act.Identity, bias=1.0, scale=0.0), eIO)
-    eJX = ev()
-    for a, b in ((0, 0), (64, 64)):
-        do(A.activation(T.JX[a:a + 64, b:b + 64], T.JJ[a:a + 64, b:b + 64], Act.Copy), eJX)
-    for a, b in ((0, 64), (64, 0)):
-        do(A.activation(T.JX[a:a + 64, b:b + 64], T.JJ[a:a + 64, b:b + 64], Act.Identity, bias=-64.0, scale=1.0), eJX)
-    wait("A", ePA, eJX)
-    e1 = do(A.activation(T.A1[:], T.JX[:], Act.Abs))
-    e2 = do(A.activation(T.A2[:], T.JX[:], Act.Abs, bias=aV, scale=-1.0))
-    e3 = do(A.activation(T.A3[:], T.JJ[:], Act.Abs, bias=pj, scale=-1.0))
-    e4 = do(A.activation(T.A4[:], T.G16[:], Act.Abs, bias=pg, scale=-1.0))
-    wait("A", e2)
-    eWb = do(A.activation(T.Wb[:], T.A2[:], Act.Relu, bias=sC, scale=sCn))
-    wait("A", e1)
-    eB = ev()
-    do(A.activation(T.W1[:], T.A1[:], Act.Relu, bias=s1, scale=sN), eB)
-    wait("A", e3)
-    eDM = do(A.activation(T.DM[:], T.A3[:], Act.Relu, bias=1.0, scale=-1.0))
-    wait("A", e4)
-    do(A.activation(T.BB[:], T.A4[:], Act.Relu, bias=512.0, scale=-512.0), eB)
-    do(A.activation(T.BF[:], T.A4[:], Act.Relu, bias=512.0, scale=-512.0), eB)
+    wait("V", ePI)
+    ePF = do(V.tensor_copy(T.PF[:, 0:6], T.PI[:, 0:6]))
 
     if r == 0:
         wait("V", eRI)
@@ -206,10 +139,65 @@ def rank_program(g, core, T, topo):
                                               srcs=[T.RB[:]], dsts=[T.RB[:] for s in others])], local_sem=T.sem.snt)
         snt["n"] += ne
         aR = eRB
-    eQLf = ev()
-    for h in range(2):
-        iota(T.QLf[:, 8 * h:8 * h + 8], [[128, 2], [4, 2], [8, 2]], 2 * h, 0, True, eQLf)
-    eRQi = iota(T.RQi[:], [[-1, 2], [1, 16]], 0, -2)
+    iota(T.G16[:], [[1, 8], [0, 16]], 0, 0, True, eJJ)
+
+    def small_iotas():
+        eT = iota(T.TR[:], [[1, 8], [8, 2], [0, 4]], 16 * r, -1)
+        eQ = ev()
+        for h in range(2):
+            iota(T.QLf[:, 8 * h:8 * h + 8], [[128, 2], [4, 2], [8, 2]], 2 * h, 0, True, eQ)
+        iota(T.RQi[:], [[-1, 2], [1, 16]], 0, -2, True, eQ)
+        return eT, eQ
+
+    def zeros():
+        e0 = do(V.memset(T.SR[0:64], 0.0))
+        return do(V.memset(T.SI[:], 0.0), e0)
+
+    def selectors(e0):
+        wait("V", eTR, e0)
+        eR = do(V.tensor_scalar(T.SR[0:64, :, 0::16], T.TR[0:64], 0.0, None, Op.is_equal))
+        eI = ev()
+        do(V.memset(T.SI[0:1, :, 1::16], 16.0), eI)
+        do(V.memset(T.SI[32:33, :, 2::16], 1.0), eI)
+        for q in range(1, 4):
+            do(V.memset(T.SI[64:65, q, 1::16], 128.0 * q), eI)
+        return eR, eI
+    if r:
+        eTR, eQLf = small_iotas()
+        eSR, eSI = selectors(zeros())
+
+    pj, pcc, pd, pg, p7, p8 = [T.PF[:, i:i + 1] for i in range(6)]
+    a0, aV, s1, sN, sV, sC, sCn, fq, sg = [T.PA[:, i:i + 1] for i in range(9)]
+    wait("A", ePF)
+    esg = do(A.activation(sg, pj, Act.Sign, bias=3.5, scale=-1.0))
+    ePA = ev()
+    do(A.activation(fq, p7, Act.Identity, bias=p8, scale=16.0), ePA)
+    do(A.activation(a0, pj, Act.Identity, bias=pcc, scale=4.0), ePA)
+    do(A.activation(aV, pcc, Act.Identity, bias=pd, scale=4.0), ePA)
+    wait("A", esg)
+    for col, sc, bi in ((s1, 0.5, 0.5), (sN, -0.5, -0.5), (sV, 256.0, 256.0), (sC, -0.5, 0.5), (sCn, 0.5, -0.5)):
+        do(A.activation(col, sg, Act.Identity, bias=bi, scale=sc), ePA)
+    wait("A", eJJ)
+    eIO = ev()
+    do(A.activation(T.IOT[0:32, :], T.G16[0:32, :], Act.Copy), eIO)
+    do(A.activation(T.IOT[32:64, :], T.JJ[32:64, :], Act.Copy), eIO)
+    do(A.activation(T.IOT[64:128, :], T.JJ[64:128, :], Act.Identity, bias=1.0, scale=0.0), eIO)
+    eJX = ev()
+    for a, b in ((0, 0), (64, 64), (0, 64), (64, 0)):
+        do(A.activation(T.JX[a:a + 64, b:b + 64], T.JJ[a:a + 64, b:b + 64], Act.Identity, bias=0.0 if a == b else -64.0), eJX)
+    e3 = do(A.activation(T.A3[:], T.JJ[:], Act.Abs, bias=pj, scale=-1.0))
+    do(A.activation(T.A4[:], T.G16[:], Act.Abs, bias=pg, scale=-1.0), e3)
+    wait("A", ePA, eJX)
+    e1 = do(A.activation(T.A2[:], T.JX[:], Act.Abs, bias=aV, scale=-1.0))
+    do(A.activation(T.A1[:], T.JX[:], Act.Abs), e1)
+    wait("A", e3)
+    eDM = do(A.activation(T.DM[:], T.A3[:], Act.Relu, bias=1.0, scale=-1.0))
+    wait("A", e1)
+    eWb = do(A.activation(T.Wb[:], T.A2[:], Act.Relu, bias=sC, scale=sCn))
+    eB = ev()
+    do(A.activation(T.W1[:], T.A1[:], Act.Relu, bias=s1, scale=sN), eB)
+    do(A.activation(T.BB[:], T.A4[:], Act.Relu, bias=512.0, scale=-512.0), eB)
+    do(A.activation(T.BF[:], T.A4[:], Act.Relu, bias=512.0, scale=-512.0), eB)
 
     wait("V", eK)
     eKF = ev()
@@ -220,32 +208,39 @@ def rank_program(g, core, T, topo):
     wait("V", e)
     eKS = do(V.tensor_copy(T.KS[:], ps[4][:, 0:128]))
     wait("g", eKS)
-    for s in others:
-        send(s, T.LL[:, 32 * r:32 * r + 32], T.KS[:, 32 * s:32 * s + 32], "aL%d" % r)
+    send(lambda s: T.LL[:, 32 * r:32 * r + 32], lambda s: T.KS[:, 32 * s:32 * s + 32], lambda s: "aL%d" % r, False)
     aL[r] = eKS
+    if r == 0:
+        eTR, eQLf = small_iotas()
+        e0 = zeros()
     eBLi = iota(T.BLi[:], [[1, 8]], 0, 0, False)
 
     wait("V", eQLf, ePA)
     eQL = do(V.tensor_scalar(T.QL[:], T.QLf[:], fq, None, Op.add))
-    wait("V", eRQi)
     eRQ = do(V.tensor_scalar(T.RQ[:], T.RQi[:], 0.0, None, Op.is_equal))
     wait("V", eQL, eQW)
     eQG = do(V.tensor_copy(T.QG[:], T.QW[:].indirect(T.QL[:])))
     if r == 0:
-        eSR, eSI = selectors()
+        eSR, eSI = selectors(e0)
 
-    def numbers():
+    even, uneven = (0, 128, 256, 384, 512), (0, 128, 256, 416, 512)
+
+    def numbers(cut):
         for q in range(4):
-            P.matmul(ps[q][:, 0:128], T.SI[:, q, :], T.IOT[:], True, False)
+            a = cut[q]
+            while a < cut[q + 1]:
+                b = min(cut[q + 1], a - a % 128 + 128)
+                P.matmul(ps[q][:, a - cut[q]:b - cut[q]], T.SI[:, a // 128, :], T.IOT[:, a % 128:a % 128 + b - a], a == cut[q], False)
+                a = b
     if r:
         wait("P", eIO, eSI)
-        numbers()
+        numbers(even)
     wait("P", eQG, eRQ)
     P.matmul(ps[5][:, 0:16], T.QG[0:8, 0:128], T.RQ[0:8, 0:16], True, False)
     e = do(P.matmul(ps[5][:, 0:16], T.QG[0:8, 128:256], T.RQ[0:8, 16:32], False, True))
     if r == 0:
         wait("P", eIO, eSI)
-        numbers()
+        numbers(even)
     wait("V", eJX)
     eW0 = do(V.tensor_scalar(T.W0[:], T.JX[:], a0, None, Op.is_equal))
     eWa = do(V.tensor_scalar(T.Wa[:], T.JX[:], aV, sV, Op.is_gt, Op.mult))
@@ -253,22 +248,22 @@ def rank_program(g, core, T, topo):
     eQS = ev()
     do(V.tensor_copy(T.QS[:], ps[5][:, 0:16]), eQS)
     do(V.tensor_copy(T.QA[:, r, 0:4], ps[5][:, 4 * r:4 * r + 4]), eQS)
-    wait("V", eWa, eWb)
-    eWV = do(V.tensor_tensor(T.WV[:], T.Wa[:], T.Wb[:], Op.add))
     wait("V", eBLi)
     eBL = do(V.tensor_copy(T.BL[:], T.BLi[:]))
+    wait("V", eWa, eWb)
+    do(V.tensor_tensor(T.WV[:], T.Wa[:], T.Wb[:], Op.subtract), eB)
     wait("g", eQS)
-    fused(lambda s: T.QA[:, r, 0:4], lambda s: T.QS[:, 4 * s:4 * s + 4], "aQ")
+    send(lambda s: T.QA[:, r, 0:4], lambda s: T.QS[:, 4 * s:4 * s + 4], lambda s: "aQ", True)
     if r == 0:
         wait("g", eLD)
-        fused(lambda s: T.LD[s], lambda s: T.LD[s], "aW")
+        send(lambda s: T.LD[s], lambda s: T.LD[s], lambda s: "aW", True)
     eLW0 = iota(T.LW[:], [[0, 512]], 0, 0, False)
     wait("Y", eLW0)
     if r:
         wait("Y", aW)
     eLW = ev()
-    for q in range(4):
-        do(Y.dma_start(T.LW[16 * q::64, :], T.LD[r] if r else T.letter[0:2, :]), eLW, 16)
+    for p in (15, 16, 47, 48):
+        do(Y.dma_start(T.LW[p::64, :], T.LD[r] if r else T.letter[0:2, :]), eLW, 16)
 
     def copy(q, out, in_, e=None):
         return do(V.tensor_copy(out, in_) if q == "V" else A.activation(out, in_, Act.Copy), e)
@@ -276,11 +271,11 @@ def rank_program(g, core, T, topo):
     order = (0, 2, 1, 3)
     eng = "VVAA"
 
-    def copies(win, banks, em, who=eng):
+    def copies(win, banks, em, cut=uneven):
         e = ev()
         for q in order:
-            wait(who[q], em[q])
-            copy(who[q], win[:, 128 * q:128 * q + 128], banks[q][:, 0:128], e)
+            wait(eng[q], em[q])
+            copy(eng[q], win[:, cut[q]:cut[q + 1]], banks[q][:, 0:cut[q + 1] - cut[q]], e)
         return e
 
     wait("P", eSR, aR)
@@ -289,25 +284,27 @@ def rank_program(g, core, T, topo):
         for b in (2 * q, 2 * q + 1):
             m = P.matmul(ps[q][:, 64 * (b % 2):64 * (b % 2) + 64], T.SR[0:64, b, :], T.RB[0:64, :], False, b % 2 == 1)
         em[q] = do(m)
-    eSY = copies(T.SY, ps[0:4], em)
+    eSY = copies(T.SY, ps[0:4], em, even)
 
     def level(h, win, ew, X, Wt, banks, first):
         lists = T.KS if h == r else T.LL
         eg = {}
         for q in order:
+            a, b = uneven[q:q + 2]
             wait(eng[q], aL[h], ew)
-            eg[q] = copy(eng[q], X[:, 128 * q:128 * q + 128], win[:].indirect(lists[:, 32 * h + 8 * q:32 * h + 8 * q + 8]))
+            eg[q] = copy(eng[q], X[:, a:b], win[:].indirect(lists[:, 32 * h + a // 16:32 * h + b // 16]))
         em = {}
         for q in order:
+            a, b = uneven[q:q + 2]
             wait("P", eg[q])
-            em[q] = do(P.matmul(banks[q][:, 0:128], Wt[:], X[:, 128 * q:128 * q + 128], first, True))
+            em[q] = do(P.matmul(banks[q][:, 0:b - a], Wt[:], X[:, a:b], first, True))
         return em
 
-    wait("P", eW0, eWV, eB, eKS, eQS)
+    wait("P", eW0, eKS, eQS)
     em = level(0, T.SY, eSY, T.X0, T.W0, ps[4:8], True)
     eT0 = copies(T.T0, ps[4:8], em)
-    wait("P", eSY)
-    numbers()
+    wait("P", eSY, eB)
+    numbers(uneven)
     em = level(1, T.T0, eT0, T.X1, T.W1, ps[0:4], False)
     eT1 = copies(T.T1, ps[0:4], em)
     wait("P", eT0)
@@ -315,26 +312,27 @@ def rank_program(g, core, T, topo):
     do(P.matmul(ps[6][:, 256:512], T.WV[:], T.X1[:, 0:256], True, True), eVm)
     do(P.matmul(ps[7][:, 256:512], T.WV[:], T.X1[:, 256:512], True, True), eVm)
     em = level(2, T.T1, eT1, T.X2, T.W0, ps[4:8], True)
-    eT2 = copies(T.T2, ps[4:8], em, "VAAA")
     wait("V", aQ, eQS)
     eO0 = do(V.tensor_copy(T.O0[:], T.QA[:, :, 2:4]))
-    eN0 = do(V.tensor_copy(T.N0[:], T.QA[:, :, 0:2]))
+    do(V.tensor_copy(T.N0[:], T.QA[:, :, 0:2]), eO0)
+    eT2 = copies(T.T2, ps[4:8], em)
     wait("V", eO0, eBL, eDM)
     eD1 = do(V.tensor_tensor(T.D1[:], T.O0[:].indirect(T.BL[:]), T.DM[:], Op.mult))
     wait("P", eT1, eT2, eD1)
     eZ = [do(P.matmul(ps[4][:, 0:64], T.BF[:], T.D1[:, 0:64], True, True))]
     em = level(3, T.T2, eT2, T.X3, T.WV, ps[0:4], True)
     eZ.append(do(P.matmul(ps[5][:, 0:64], T.BF[:], T.D1[:, 64:128], True, True)))
+    wait("A", eO0)
     eV3 = copies(T.V3, ps[0:4], em)
 
     H = (slice(0, 64), slice(64, 128))
 
     def pick(k, eG, eZ, z):
-        G, TA, TT, M, SC, UI, NI, N = [T["%s_%d" % (n, k)] for n in ("G", "TA", "TT", "M", "SC", "UI", "NI", "N")]
+        G, TA, TT, M, SC, NI, N = [T["%s_%d" % (n, k)] for n in ("G", "TA", "TT", "M", "SC", "NI", "N")]
         e = [None, None]
         for h in range(2):
-            wait("V", eG[h], eZ[h])
-            e[h] = do(V.tensor_tensor(TA[:, H[h]], G[:, H[h]], z[h][:, 0:64], Op.add))
+            wait("V", eZ[h], eG[h])
+            e[h] = do(V.tensor_tensor(TA[:, H[h]], z[h][:, 0:64], G[:, H[h]], Op.subtract))
         for h in range(2):
             wait("V", e[h])
             e[h] = do(V.transpose(TT[:, H[h]], TA[:, H[h]]))
@@ -346,18 +344,17 @@ def rank_program(g, core, T, topo):
             wait("V", e[h])
             do(V.tensor_tensor_scan(SC[:, H[h]], M[:, H[h]], TT[:, H[h]], 0.0, Op.mult, Op.max), eS)
         wait("V", eS)
-        eU = do(V.tensor_copy(UI[:], SC[:, 15::16]))
-        wait("V", eU)
-        e = do(V.tensor_scalar(NI[:], UI[:], 511, None, Op.bitwise_and))
-        eO = do(V.tensor_scalar(T.OI[:], UI[:], 9, None, Op.logical_shift_right)) if k == 1 else None
+        U = SC[:, 15::16]
+        e = do(V.tensor_scalar(NI[:], U, 511, None, band))
+        eO = do(V.tensor_scalar(T.OI[:], U, 9, None, shr)) if k == 1 else None
         wait("V", e)
         return do(V.tensor_copy(N[:], NI[:])), eO
 
-    wait("V", eV3, eN0)
-    wait("A", eV3, eN0)
+    wait("V", eV3)
+    wait("A", eV3)
     eG = [copy("VA"[h], T.G_1[:, H[h]], T.V3[:].indirect(T.N0[:, 4 * h:4 * h + 4])) for h in range(2)]
     eV1 = ev()
-    wait("A", eVm, eT2)
+    wait("A", eVm)
     copy("A", T.V1[:, 0:256], ps[6][:, 256:512], eV1)
     copy("A", T.V1[:, 256:512], ps[7][:, 256:512], eV1)
     eN, eO = pick(1, eG, eZ, ps[4:6])
@@ -372,25 +369,23 @@ def rank_program(g, core, T, topo):
         eZ.append(do(P.matmul(ps[h][:, 0:64], T.BB[:], T.D2[:, H[h]], True, True)))
     eN, _ = pick(2, eG, eZ, ps[0:2])
     wait("V", eLW, eN)
-    e = do(V.tensor_copy(T.LG[:], T.LW[:].indirect(T.N_2[:])))
-    wait("V", e)
-    e = do(V.transpose(T.LT[:], T.LG[:]))
-    wait("V", e)
-    eAN = do(V.tensor_copy(T.AN[:], T.LT[:, 0::16]))
-    wait("g", eAN)
-    for s in others:
-        send(s, T.AD[r], T.AN[:, 2 * s:2 * s + 2], "aLo" if r < s else "aHi")
+    parts = (1 - r // 2, r // 2)
+    eL = [do(V.tensor_copy(T.LG[:, H[h]], T.LW[:].indirect(T.N_2[:, 4 * h:4 * h + 4]))) for h in parts]
+    for h, e in zip(parts, eL):
+        wait("V", e)
+        eAN = do(V.transpose(T.LT[:, H[h]], T.LG[:, H[h]]))
+        wait("g", eAN)
+        send(lambda s: T.AD[r], lambda s: T.LT[:, 32 * s + 15:32 * s + 17], lambda s: "aLo" if r < s else "aHi", False,
+             range(2 * h, 2 * h + 2))
     wait("Y", eAN)
-    eY = do(Y.dma_start(T.y[2 * r:2 * r + 2, :], T.AN[:, 2 * r:2 * r + 2]), None, 16)
+    eY = do(Y.dma_start(T.y[2 * r:2 * r + 2, :], T.LT[:, 32 * r + 15:32 * r + 17]), None, 16)
     if r > 0:
         wait("A", aLo)
-        e = do(A.dma_start(T.y[0:2 * r, :], T.AD[0:r]), None, 16)
-        wait("A", e)
+        wait("A", do(A.dma_start(T.y[0:2 * r, :], T.AD[0:r]), None, 16))
     if r < 3:
         q = "Y" if r > 0 else "A"
         wait(q, aHi)
-        e = do(names[q].dma_start(T.y[2 * r + 2:8, :], T.AD[r + 1:4]), None, 16)
-        wait(q, e)
+        wait(q, do(names[q].dma_start(T.y[2 * r + 2:8, :], T.AD[r + 1:4]), None, 16))
     wait("Y", eY)
     for e in events:
         if e["n"] and e["n"] not in e["seen"].values():

from concourse.bass import DstId, RemoteDMATransfer
from concourse.mybir import AluOpType as Op, ActivationFunctionType as Act

S = "sbuf"
SCRATCH = {
    "KI": (S, [128, 2, 16, 4], "int32"), "KF": (S, [128, 2, 4, 16], "float16"), "ID": (S, [128, 128], "float16"),
    "KS": (S, [128, 128], "uint16"), "LL": (S, [128, 128], "uint16"),
    "RI": (S, [64, 64], "int32"), "RB": (S, [128, 64], "bfloat16"),
    "QW": (S, [128, 256], "int32"), "QG": (S, [128, 256], "float32"), "QLf": (S, [128, 16], "float32"),
    "QL": (S, [128, 16], "uint16"), "RQi": (S, [128, 32], "float32"), "RQ": (S, [128, 32], "float32"),
    "QS": (S, [128, 16], "uint16"), "QA": (S, [128, 4, 8], "uint16"),
    "PC": (S, [128, 4], "int32"), "PI": (S, [128, 8], "int32"), "PF": (S, [128, 8], "float32"), "PA": (S, [128, 12], "float32"),
    "TR": (S, [128, 8, 8], "float32"), "BLi": (S, [128, 8], "int32"), "BL": (S, [128, 8], "uint16"),
    "SI": (S, [128, 4, 128], "bfloat16"), "SR": (S, [128, 8, 128], "bfloat16"),
    "LW": (S, [128, 512], "int32"), "LD": ("dram", [4, 128, 8], "int32"), "AD": ("dram", [4, 128, 2], "float32"),
    "N0": (S, [128, 8], "uint16"), "O0": (S, [128, 8], "float32"), "OI": (S, [128, 8], "int32"),
}
for _n in "JX IOT JJ G16 W0 W1 WV Wa Wb A1 A2 A3 A4 BB D2".split():
    SCRATCH[_n] = (S, [128, 128], "bfloat16")
for _n in "DI DM BF D1 LG LT G_1 TA_1 TT_1 M_1 G_2 TA_2 TT_2 M_2".split():
    SCRATCH[_n] = (S, [128, 128], "float32")
for _n in "SY T0 T1 T2 V3 V1".split():
    SCRATCH[_n] = (S, [128, 512], "float32")
for _n in "X0 X1 X2 X3".split():
    SCRATCH[_n] = (S, [128, 512], "bfloat16")
for _k in (1, 2):
    SCRATCH["SC_%d" % _k] = (S, [128, 128], "int32")
    SCRATCH["NI_%d" % _k] = (S, [128, 8], "int32")
    SCRATCH["N_%d" % _k] = (S, [128, 8], "uint16")
for _k in range(8):
    SCRATCH["ps%d" % _k] = ("psum", [128, 512], "float32")
SEMAPHORES = ["aL0", "aL1", "aL2", "aL3", "aR", "aQ", "aW", "aLo", "aHi", "snt"] + ["s%d" % _k for _k in range(140)]


def rank_program(g, core, T, topo):
    r = T.rank_of(core)
    if r is None:
        return
    cores = T.cores
    V, A, P, Y = g.vector, g.scalar, g.tensor, g.sync
    names = {"g": g, "V": V, "A": A, "P": P, "Y": Y}
    events = []

    def ev(name=None, count=0):
        auto = name is None
        if auto:
            name = "s%d" % len([e for e in events if e["auto"]])
        events.append({"sem": T.sem[name], "n": count, "auto": auto, "seen": {}})
        return events[-1]

    def do(inst, e=None, n=1):
        if e is None:
            e = ev()
        inst.then_inc(e["sem"], n)
        e["n"] += n
        return e

    def wait(q, *es):
        for e in es:
            if e["seen"].get(q) != e["n"]:
                names[q].wait_ge(e["sem"], e["n"])
                e["seen"][q] = e["n"]

    def iota(out, pattern, base, cm, flag=True, e=None):
        kw = dict(allow_small_or_imprecise_dtypes=True) if flag else {}
        return do(g.iota(out, pattern, base, cm, **kw), e)

    ps = [T["ps%d" % k] for k in range(8)]

    def far_first(f):
        a = topo.chip(cores[f])
        near = lambda s: topo.mates(a, topo.chip(cores[s])) or topo.same_plane(a, topo.chip(cores[s]))
        return sorted([s for s in range(4) if s != f], key=near)
    others = far_first(r)
    ne = len(topo.engines(core, cores[others[0]]))
    snt = ev("snt")

    def shares(f):
        cut = [(0, ne // 2), (ne // 2, 3 * ne // 4), (3 * ne // 4, ne)]
        return {s: topo.engines(cores[f], cores[s])[cut[i][0]:cut[i][1]] for i, s in enumerate(far_first(f))}

    def send(dst_of, src_of, sem_of, fuse, only=range(4)):
        tr = []
        for s, en in shares(r).items():
            if s not in only:
                continue
            rid, pid, _ = topo.addr(cores[s])
            if fuse:
                tr.append(RemoteDMATransfer(dst_ids=[DstId(rid=rid, pnc=pid)], dma_engine_mask=sum(1 << e for e in en),
                                            remote_sem=T.sem[sem_of(s)], src=src_of(s), dst=dst_of(s)))
            else:
                g.remote_dma(dst_of(s), src_of(s), T.sem[sem_of(s)], T.sem.snt, pid, rid, topo.mask(core, cores[s]))
            snt["n"] += len(en) if fuse else ne
        if fuse:
            g.remote_dma_fused(tr, local_sem=T.sem.snt)

    aL = [ev("aL%d" % s, ne) if s != r else None for s in range(4)]
    aR = ev("aR", ne) if r else None
    aQ = ev("aQ", sum(len(shares(s)[r]) for s in others))
    aW = ev("aW", len(shares(0)[r])) if r else None
    aLo = ev("aLo", ne * r)
    aHi = ev("aHi", ne * (3 - r))

    eK = ev()
    if r == 0:
        eRI = do(Y.dma_start(T.RI[:], T.runs[:]), None, 16)
        eRB = do(V.memset(T.RB[64:128, :], 0.0))
    do(Y.dma_start(T.KI[:, 0], T.kids[0::2, :]), eK, 16)
    do(A.dma_start(T.KI[:, 1], T.kids[1::2, :]), eK, 16)
    eQW0 = do(V.memset(T.QW[:], 0))
    wait("Y", eQW0)
    eQW = ev()
    do(Y.dma_start(T.QW[0:8:2, :], T.top[:]), eQW, 16)
    do(Y.dma_start(T.QW[1:8:2, :], T.off[:]), eQW, 16)
    if r == 0:
        eLD = do(Y.dma_start(T.LD[:], T.letter[:]), None, 16)

    ePC = iota(T.PC[:, 0:1], [[0, 1]], 0, 1, False)
    eDI = iota(T.DI[:], [[1, 128]], 0, -1)
    eJJ = iota(T.JJ[:], [[0, 8], [1, 16]], 0, 0)

    wait("V", ePC)
    ePI = ev()
    pc = T.PC[:, 0:1]
    shr, band = Op.logical_shift_right, Op.bitwise_and
    for i, a in enumerate(((15, None, band), (4, 3, shr, band), (3, None, band), (4, None, shr), (7, None, band), (3, 1, shr, band))):
        do(V.tensor_scalar(T.PI[:, i:i + 1], pc, *a), ePI)
    wait("V", eDI)
    eID = do(V.tensor_scalar(T.ID[:], T.DI[:], 0.0, None, Op.is_equal))
    wait("V", ePI)
    ePF = do(V.tensor_copy(T.PF[:, 0:6], T.PI[:, 0:6]))

    if r == 0:
        wait("V", eRI)
        do(V.tensor_copy(T.RB[0:64, :], T.RI[:]), eRB)
        wait("g", eRB)
        ids = [DstId(rid=topo.addr(cores[s])[0], pnc=topo.addr(cores[s])[1]) for s in others]
        g.remote_dma_fused([RemoteDMATransfer(dst_ids=ids, dma_engine_mask=topo.mask(core, cores[others[0]]), remote_sem=T.sem.aR,
                                              srcs=[T.RB[:]], dsts=[T.RB[:] for s in others])], local_sem=T.sem.snt)
        snt["n"] += ne
        aR = eRB
    iota(T.G16[:], [[1, 8], [0, 16]], 0, 0, True, eJJ)

    def small_iotas():
        eT = iota(T.TR[:], [[1, 8], [8, 2], [0, 4]], 16 * r, -1)
        eQ = ev()
        for h in range(2):
            iota(T.QLf[:, 8 * h:8 * h + 8], [[128, 2], [4, 2], [8, 2]], 2 * h, 0, True, eQ)
        iota(T.RQi[:], [[-1, 2], [1, 16]], 0, -2, True, eQ)
        return eT, eQ

    def zeros():
        e0 = do(V.memset(T.SR[0:64], 0.0))
        return do(V.memset(T.SI[:], 0.0), e0)

    def selectors(e0):
        wait("V", eTR, e0)
        eR = do(V.tensor_scalar(T.SR[0:64, :, 0::16], T.TR[0:64], 0.0, None, Op.is_equal))
        eI = ev()
        do(V.memset(T.SI[0:1, :, 1::16], 16.0), eI)
        do(V.memset(T.SI[32:33, :, 2::16], 1.0), eI)
        for q in range(1, 4):
            do(V.memset(T.SI[64:65, q, 1::16], 128.0 * q), eI)
        return eR, eI
    if r:
        eTR, eQLf = small_iotas()
        eSR, eSI = selectors(zeros())

    pj, pcc, pd, pg, p7, p8 = [T.PF[:, i:i + 1] for i in range(6)]
    a0, aV, s1, sN, sV, sC, sCn, fq, sg = [T.PA[:, i:i + 1] for i in range(9)]
    wait("A", ePF)
    esg = do(A.activation(sg, pj, Act.Sign, bias=3.5, scale=-1.0))
    ePA = ev()
    do(A.activation(fq, p7, Act.Identity, bias=p8, scale=16.0), ePA)
    do(A.activation(a0, pj, Act.Identity, bias=pcc, scale=4.0), ePA)
    do(A.activation(aV, pcc, Act.Identity, bias=pd, scale=4.0), ePA)
    wait("A", esg)
    for col, sc, bi in ((s1, 0.5, 0.5), (sN, -0.5, -0.5), (sV, 256.0, 256.0), (sC, -0.5, 0.5), (sCn, 0.5, -0.5)):
        do(A.activation(col, sg, Act.Identity, bias=bi, scale=sc), ePA)
    wait("A", eJJ)
    eIO = ev()
    do(A.activation(T.IOT[0:32, :], T.G16[0:32, :], Act.Copy), eIO)
    do(A.activation(T.IOT[32:64, :], T.JJ[32:64, :], Act.Copy), eIO)
    do(A.activation(T.IOT[64:128, :], T.JJ[64:128, :], Act.Identity, bias=1.0, scale=0.0), eIO)
    eJX = ev()
    for a, b in ((0, 0), (64, 64), (0, 64), (64, 0)):
        do(A.activation(T.JX[a:a + 64, b:b + 64], T.JJ[a:a + 64, b:b + 64], Act.Identity, bias=0.0 if a == b else -64.0), eJX)
    e3 = do(A.activation(T.A3[:], T.JJ[:], Act.Abs, bias=pj, scale=-1.0))
    do(A.activation(T.A4[:], T.G16[:], Act.Abs, bias=pg, scale=-1.0), e3)
    wait("A", ePA, eJX)
    e1 = do(A.activation(T.A2[:], T.JX[:], Act.Abs, bias=aV, scale=-1.0))
    do(A.activation(T.A1[:], T.JX[:], Act.Abs), e1)
    wait("A", e3)
    eDM = do(A.activation(T.DM[:], T.A3[:], Act.Relu, bias=1.0, scale=-1.0))
    wait("A", e1)
    eWb = do(A.activation(T.Wb[:], T.A2[:], Act.Relu, bias=sC, scale=sCn))
    eB = ev()
    do(A.activation(T.W1[:], T.A1[:], Act.Relu, bias=s1, scale=sN), eB)
    do(A.activation(T.BB[:], T.A4[:], Act.Relu, bias=512.0, scale=-512.0), eB)
    do(A.activation(T.BF[:], T.A4[:], Act.Relu, bias=512.0, scale=-512.0), eB)

    wait("V", eK)
    eKF = ev()
    for c in range(4):
        do(V.tensor_copy(T.KF[:, :, c, :], T.KI[:, :, :, c]), eKF)
    wait("P", eID, eKF)
    e = do(P.matmul(ps[4][:, 0:128], T.KF[:], T.ID[:], True, True))
    wait("V", e)
    eKS = do(V.tensor_copy(T.KS[:], ps[4][:, 0:128]))
    wait("g", eKS)
    send(lambda s: T.LL[:, 32 * r:32 * r + 32], lambda s: T.KS[:, 32 * s:32 * s + 32], lambda s: "aL%d" % r, False)
    aL[r] = eKS
    if r == 0:
        eTR, eQLf = small_iotas()
        e0 = zeros()
    eBLi = iota(T.BLi[:], [[1, 8]], 0, 0, False)

    wait("V", eQLf, ePA)
    eQL = do(V.tensor_scalar(T.QL[:], T.QLf[:], fq, None, Op.add))
    eRQ = do(V.tensor_scalar(T.RQ[:], T.RQi[:], 0.0, None, Op.is_equal))
    wait("V", eQL, eQW)
    eQG = do(V.tensor_copy(T.QG[:], T.QW[:].indirect(T.QL[:])))
    if r == 0:
        eSR, eSI = selectors(e0)

    even, uneven = (0, 128, 256, 384, 512), (0, 128, 256, 416, 512)

    def numbers(cut):
        for q in range(4):
            a = cut[q]
            while a < cut[q + 1]:
                b = min(cut[q + 1], a - a % 128 + 128)
                P.matmul(ps[q][:, a - cut[q]:b - cut[q]], T.SI[:, a // 128, :], T.IOT[:, a % 128:a % 128 + b - a], a == cut[q], False)
                a = b
    if r:
        wait("P", eIO, eSI)
        numbers(even)
    wait("P", eQG, eRQ)
    P.matmul(ps[5][:, 0:16], T.QG[0:8, 0:128], T.RQ[0:8, 0:16], True, False)
    e = do(P.matmul(ps[5][:, 0:16], T.QG[0:8, 128:256], T.RQ[0:8, 16:32], False, True))
    if r == 0:
        wait("P", eIO, eSI)
        numbers(even)
    wait("V", eJX)
    eW0 = do(V.tensor_scalar(T.W0[:], T.JX[:], a0, None, Op.is_equal))
    eWa = do(V.tensor_scalar(T.Wa[:], T.JX[:], aV, sV, Op.is_gt, Op.mult))
    wait("V", e)
    eQS = ev()
    do(V.tensor_copy(T.QS[:], ps[5][:, 0:16]), eQS)
    do(V.tensor_copy(T.QA[:, r, 0:4], ps[5][:, 4 * r:4 * r + 4]), eQS)
    wait("V", eBLi)
    eBL = do(V.tensor_copy(T.BL[:], T.BLi[:]))
    wait("V", eWa, eWb)
    do(V.tensor_tensor(T.WV[:], T.Wa[:], T.Wb[:], Op.subtract), eB)
    wait("g", eQS)
    send(lambda s: T.QA[:, r, 0:4], lambda s: T.QS[:, 4 * s:4 * s + 4], lambda s: "aQ", True)
    if r == 0:
        wait("g", eLD)
        send(lambda s: T.LD[s], lambda s: T.LD[s], lambda s: "aW", True)
    eLW0 = iota(T.LW[:], [[0, 512]], 0, 0, False)
    wait("Y", eLW0)
    if r:
        wait("Y", aW)
    eLW = ev()
    for p in (15, 16, 47, 48):
        do(Y.dma_start(T.LW[p::64, :], T.LD[r] if r else T.letter[0:2, :]), eLW, 16)

    def copy(q, out, in_, e=None):
        return do(V.tensor_copy(out, in_) if q == "V" else A.activation(out, in_, Act.Copy), e)

    order = (0, 2, 1, 3)
    eng = "VVAA"

    def copies(win, banks, em, cut=uneven):
        e = ev()
        for q in order:
            wait(eng[q], em[q])
            copy(eng[q], win[:, cut[q]:cut[q + 1]], banks[q][:, 0:cut[q + 1] - cut[q]], e)
        return e

    wait("P", eSR, aR)
    em = {}
    for q in order:
        for b in (2 * q, 2 * q + 1):
            m = P.matmul(ps[q][:, 64 * (b % 2):64 * (b % 2) + 64], T.SR[0:64, b, :], T.RB[0:64, :], False, b % 2 == 1)
        em[q] = do(m)
    eSY = copies(T.SY, ps[0:4], em, even)

    def level(h, win, ew, X, Wt, banks, first):
        lists = T.KS if h == r else T.LL
        eg = {}
        for q in order:
            a, b = uneven[q:q + 2]
            wait(eng[q], aL[h], ew)
            eg[q] = copy(eng[q], X[:, a:b], win[:].indirect(lists[:, 32 * h + a // 16:32 * h + b // 16]))
        em = {}
        for q in order:
            a, b = uneven[q:q + 2]
            wait("P", eg[q])
            em[q] = do(P.matmul(banks[q][:, 0:b - a], Wt[:], X[:, a:b], first, True))
        return em

    wait("P", eW0, eKS, eQS)
    em = level(0, T.SY, eSY, T.X0, T.W0, ps[4:8], True)
    eT0 = copies(T.T0, ps[4:8], em)
    wait("P", eSY, eB)
    numbers(uneven)
    em = level(1, T.T0, eT0, T.X1, T.W1, ps[0:4], False)
    eT1 = copies(T.T1, ps[0:4], em)
    wait("P", eT0)
    eVm = ev()
    do(P.matmul(ps[6][:, 256:512], T.WV[:], T.X1[:, 0:256], True, True), eVm)
    do(P.matmul(ps[7][:, 256:512], T.WV[:], T.X1[:, 256:512], True, True), eVm)
    em = level(2, T.T1, eT1, T.X2, T.W0, ps[4:8], True)
    wait("V", aQ, eQS)
    eO0 = do(V.tensor_copy(T.O0[:], T.QA[:, :, 2:4]))
    do(V.tensor_copy(T.N0[:], T.QA[:, :, 0:2]), eO0)
    eT2 = copies(T.T2, ps[4:8], em)
    wait("V", eO0, eBL, eDM)
    eD1 = do(V.tensor_tensor(T.D1[:], T.O0[:].indirect(T.BL[:]), T.DM[:], Op.mult))
    wait("P", eT1, eT2, eD1)
    eZ = [do(P.matmul(ps[4][:, 0:64], T.BF[:], T.D1[:, 0:64], True, True))]
    em = level(3, T.T2, eT2, T.X3, T.WV, ps[0:4], True)
    eZ.append(do(P.matmul(ps[5][:, 0:64], T.BF[:], T.D1[:, 64:128], True, True)))
    wait("A", eO0)
    eV3 = copies(T.V3, ps[0:4], em)

    H = (slice(0, 64), slice(64, 128))

    def pick(k, eG, eZ, z):
        G, TA, TT, M, SC, NI, N = [T["%s_%d" % (n, k)] for n in ("G", "TA", "TT", "M", "SC", "NI", "N")]
        e = [None, None]
        for h in range(2):
            wait("V", eZ[h], eG[h])
            e[h] = do(V.tensor_tensor(TA[:, H[h]], z[h][:, 0:64], G[:, H[h]], Op.subtract))
        for h in range(2):
            wait("V", e[h])
            e[h] = do(V.transpose(TT[:, H[h]], TA[:, H[h]]))
        for h in range(2):
            wait("V", e[h])
            e[h] = do(V.tensor_scalar(M[:, H[h]], TT[:, H[h]], 0.0, None, Op.is_lt))
        eS = ev()
        for h in range(2):
            wait("V", e[h])
            do(V.tensor_tensor_scan(SC[:, H[h]], M[:, H[h]], TT[:, H[h]], 0.0, Op.mult, Op.max), eS)
        wait("V", eS)
        U = SC[:, 15::16]
        e = do(V.tensor_scalar(NI[:], U, 511, None, band))
        eO = do(V.tensor_scalar(T.OI[:], U, 9, None, shr)) if k == 1 else None
        wait("V", e)
        return do(V.tensor_copy(N[:], NI[:])), eO

    wait("V", eV3)
    wait("A", eV3)
    eG = [copy("VA"[h], T.G_1[:, H[h]], T.V3[:].indirect(T.N0[:, 4 * h:4 * h + 4])) for h in range(2)]
    eV1 = ev()
    wait("A", eVm)
    copy("A", T.V1[:, 0:256], ps[6][:, 256:512], eV1)
    copy("A", T.V1[:, 256:512], ps[7][:, 256:512], eV1)
    eN, eO = pick(1, eG, eZ, ps[4:6])
    wait("A", eV1, eN)
    eG = [copy("A", T.G_2[:, H[h]], T.V1[:].indirect(T.N_1[:, 4 * h:4 * h + 4])) for h in range(2)]
    wait("V", eO)
    wait("P", eV3)
    eZ = []
    for h in range(2):
        e = do(V.tensor_tensor(T.D2[:, H[h]], T.OI[:].indirect(T.BL[:, 4 * h:4 * h + 4]), T.DM[:, H[h]], Op.mult))
        wait("P", e)
        eZ.append(do(P.matmul(ps[h][:, 0:64], T.BB[:], T.D2[:, H[h]], True, True)))
    eN, _ = pick(2, eG, eZ, ps[0:2])
    wait("V", eLW, eN)
    parts = (1 - r // 2, r // 2)
    eL = [do(V.tensor_copy(T.LG[:, H[h]], T.LW[:].indirect(T.N_2[:, 4 * h:4 * h + 4]))) for h in parts]
    for h, e in zip(parts, eL):
        wait("V", e)
        eAN = do(V.transpose(T.LT[:, H[h]], T.LG[:, H[h]]))
        wait("g", eAN)
        send(lambda s: T.AD[r], lambda s: T.LT[:, 32 * s + 15:32 * s + 17], lambda s: "aLo" if r < s else "aHi", False,
             range(2 * h, 2 * h + 2))
    wait("Y", eAN)
    eY = do(Y.dma_start(T.y[2 * r:2 * r + 2, :], T.LT[:, 32 * r + 15:32 * r + 17]), None, 16)
    if r > 0:
        wait("A", aLo)
        wait("A", do(A.dma_start(T.y[0:2 * r, :], T.AD[0:r]), None, 16))
    if r < 3:
        q = "Y" if r > 0 else "A"
        wait(q, aHi)
        wait(q, do(names[q].dma_start(T.y[2 * r + 2:8, :], T.AD[r + 1:4]), None, 16))
    wait("Y", eY)
    for e in events:
        if e["n"] and e["n"] not in e["seen"].values():
            wait("g", e)
